import numpy as np
import ml_dtypes


def mxq(x, axis, fmt="e4m3"):
    dtype, down = {"e4m3": (ml_dtypes.float8_e4m3fn, 7), "e5m2": (ml_dtypes.float8_e5m2, 14)}[fmt]
    v = np.moveaxis(np.asarray(x, np.float32).astype(ml_dtypes.bfloat16).astype(np.float64), axis, -1)
    blocks = v.reshape(v.shape[:-1] + (-1, 32))
    amax = np.abs(blocks).max(-1, keepdims=True)
    byte = np.maximum(np.where(amax > 0, np.frexp(amax)[1] - 1 + 127, 0) - down, 1)
    scale = np.exp2(byte - 127.0)
    codes = (blocks / scale).astype(np.float32).astype(dtype).astype(np.float64)
    return np.moveaxis((codes * scale).reshape(v.shape), -1, axis)


WIDE = False


def mx_kscale(k):
    if not WIDE:
        return np.ones(k)
    levels = np.array([10, -10, 5, -5, 0])
    if k % 512:
        return np.exp2(np.random.permutation(np.resize(levels, k // 32))).repeat(32)
    a = np.empty((k // 512, 16))
    for p in range(k // 512):
        a[p, :8] = np.random.permutation(np.resize(levels, 8))
        for g in range(8):
            far = levels[np.abs(levels - a[p, g]) >= 10]
            a[p, g + 8] = far[np.random.randint(len(far))]
    return np.exp2(a.ravel()).repeat(32)


def f64(x):
    return np.asarray(x).astype(np.float64)


def striped(idx):
    return np.tile(idx.reshape(-1, 16).T, (8, 1)).astype(np.uint16)


def unstriped(offs):
    return offs[:16].T.reshape(-1).astype(np.int64)


def pack_weight(w):
    k, n = w.shape
    w = f64(np.asarray(w, np.float32).astype(ml_dtypes.bfloat16)).reshape(k // 32, 32, n)
    amax = np.abs(w).max(1)
    byte = np.clip(np.where(amax > 0, np.frexp(amax)[1] - 1 + 127 - 7, 1), 1, 254)
    scaled = (w * np.exp2(127.0 - byte)[:, None, :]).reshape(k, n).astype(np.float32)
    words = np.ascontiguousarray(scaled.reshape(k // 512, 128, 4, n).transpose(0, 1, 3, 2)).astype(ml_dtypes.float8_e4m3fn).view(np.uint8)
    return words, np.ascontiguousarray(byte.astype(np.uint8).reshape(k // 512, 16, n))


def unpack_weight(words, scales):
    g, p, n, _ = words.shape
    vals = np.ascontiguousarray(words).view(ml_dtypes.float8_e4m3fn).astype(np.float64) * np.repeat(np.exp2(scales.astype(np.float64) - 127.0), 8, axis=1)[..., None]
    return vals.transpose(0, 1, 3, 2).reshape(g * 512, n)


def relu(v):
    return np.maximum(v, 0.0)


K, T, S, N, U = 512, 2048, 512, 128, 512
P = 2 ** 7


def setup_inputs():
    n = np.random.standard_normal
    s = mx_kscale(K)[:, None]
    packed_xT = pack_weight(n((K, T)) * s)
    return {
        "x_words": packed_xT[0],
        "x_scales": packed_xT[1],
        "w1": (n((K, N)) / np.sqrt(K) / s).astype(np.float32),
        "half": (np.tile(np.random.uniform(0.7, 1.3, U), (P, 1))).astype(np.float32),
        "lx": (np.random.uniform(-1.0, 1.0, (N, 1))).astype(np.float32),
        "ly": (np.random.uniform(-1.0, 1.0, (N, 1))).astype(np.float32),
        "offs": striped(np.random.permutation(T)[:S]),
        "xp": striped(np.random.permutation(S)),
        "xm": striped(np.random.permutation(S)),
        "yp": striped(np.random.permutation(S)),
        "ym": striped(np.random.permutation(S)),
    }


def reference(x_words, x_scales, w1, half, lx, ly, offs, xp, xm, yp, ym):
    xq = unpack_weight(x_words, x_scales)[:, unstriped(offs)]
    y = mxq(f64(w1), 0, "e4m3").T @ xq
    gx = f64(half)[:1] * (y[:, unstriped(xp)] - y[:, unstriped(xm)])
    gy = f64(half)[:1] * (y[:, unstriped(yp)] - y[:, unstriped(ym)])
    ln = np.sqrt((gx) ** 2 + (gy) ** 2 + 0.1)
    nx = gx / ln
    ny = gy / ln
    return relu(f64(lx) * nx + f64(ly) * ny) + 0.3 * ((relu(ny)) ** 2)

@@ -1,0 +1,149 @@
+import math
+from contextlib import ExitStack
+
+import concourse.mybir as mybir
+
+F32 = mybir.dt.float32
+BF16 = mybir.dt.bfloat16
+I32 = mybir.dt.int32
+U32 = mybir.dt.uint32
+U16 = mybir.dt.uint16
+U8 = mybir.dt.uint8
+FP8X4 = mybir.dt.float8_e4m3fn_x4
+ALU = mybir.AluOpType
+ACT = mybir.ActivationFunctionType
+
+P = 128
+K, T, S, N = 512, 2048, 512, 128
+PACK = 4
+HALF = S // 2
+FLOPS = 2 * K * S * N
+
+
+def tile_picked_ysdfnr_shade_p_kernel(
+    tc, x_words, x_scales, w1, half, lx, ly, offs, xp, xm, yp, ym, out
+):
+    nc = tc.nc
+    with ExitStack() as ctx:
+        lists = ctx.enter_context(tc.tile_pool(name="lists", bufs=1))
+        sb = ctx.enter_context(tc.tile_pool(name="sb", bufs=1))
+        ps = ctx.enter_context(tc.psum_pool(name="ps", bufs=1))
+
+        offs_t = lists.tile([P, S // 16], U16, name="offs_t")
+        ym_t = lists.tile([P, S // 16], U16, name="ym_t")
+        yp_t = lists.tile([P, S // 16], U16, name="yp_t")
+        xm_t = lists.tile([P, S // 16], U16, name="xm_t")
+        xp_t = lists.tile([P, S // 16], U16, name="xp_t")
+
+        scales = sb.tile([P, T], U8, name="scales", align_bytes=64)
+        words = sb.tile([P, T], I32, name="words", align_bytes=64)
+        w_raw = sb.tile([P, PACK, N], F32, name="w_raw")
+        h = sb.tile([P, S], F32, name="h")
+        lx_t = sb.tile([P, 1], F32, name="lx_t")
+        ly_t = sb.tile([P, 1], F32, name="ly_t")
+        y = sb.tile([P, 2 * S], F32, name="y")
+
+        zero_view = scales[:].bitcast(I32)
+        nc.vector.memset(zero_view[:, : T // 8], 0)
+        nc.gpsimd.memset(zero_view[:, T // 8 :], 0)
+        nc.sync.dma_start(out=offs_t[:], in_=offs)
+        nc.scalar.dma_start(out=w_raw[:], in_=w1.rearrange("(p j) m -> p j m", j=PACK))
+        nc.scalar.dma_start(out=words[:], in_=x_words[0].rearrange("p n t -> p (n t)").bitcast(I32))
+        for q in range(4):
+            nc.sync.dma_start(
+                out=scales[32 * q : 32 * q + 4, :].bitcast(I32),
+                in_=x_scales[0, 4 * q : 4 * q + 4, :].bitcast(I32),
+            )
+        nc.sync.dma_start(out=ym_t[:], in_=ym)
+        nc.sync.dma_start(out=yp_t[:], in_=yp)
+        nc.sync.dma_start(out=xm_t[:], in_=xm)
+        nc.sync.dma_start(out=h[:], in_=half)
+        nc.sync.dma_start(out=ly_t[:], in_=ly)
+        nc.sync.dma_start(out=xp_t[:], in_=xp)
+        nc.sync.dma_start(out=lx_t[:], in_=lx)
+        nc.vector.memset(y[:, S:], 0.0)
+
+        one = sb.tile([P, 1], F32, name="one")
+        warm = sb.tile([P, 1], F32, name="warm")
+        nc.vector.memset(one[:], 1.0)
+        nc.scalar.activation(out=warm[:], in_=one[:], func=ACT.Abs_reciprocal_sqrt)
+
+        w_bf = sb.tile([P, N, PACK], BF16, name="w_bf", align_bytes=64)
+        nc.scalar.copy(out=w_bf[:], in_=w_raw[:].rearrange("p j m -> p m j"))
+
+        g_scales = sb.tile([P, S], U8, name="g_scales", align_bytes=64)
+        nc.vector.tensor_copy(out=g_scales[:], in_=scales[:].indirect(offs_t[:]))
+
+        w_codes = sb.tile([P, N], U32, name="w_codes", align_bytes=64)
+        w_scales = sb.tile([P, N], U8, name="w_scales", align_bytes=64)
+        nc.vector.quantize_mx(
+            out=w_codes[:].bitcast(FP8X4), scales=w_scales[:], in_=w_bf[:].rearrange("p m j -> p (m j)")
+        )
+
+        for c in range(2):
+            cols = slice(c * HALF, (c + 1) * HALF)
+            g_words = sb.tile([P, HALF], U32, name="g_words%d" % c, align_bytes=64)
+            nc.vector.tensor_copy(
+                out=g_words[:], in_=words[:].bitcast(U32).indirect(offs_t[:, c * HALF // 16 : (c + 1) * HALF // 16])
+            )
+            acc = ps.tile([P, HALF], F32, name="acc%d" % c)
+            nc.tensor.matmul_mx(
+                out=acc[:],
+                lhsT=w_codes[:].bitcast(FP8X4),
+                lhsT_scale=w_scales[:],
+                rhs=g_words[:].bitcast(FP8X4),
+                rhs_scale=g_scales[:, cols],
+                start=True,
+                stop=True,
+            )
+            nc.scalar.copy(out=y[:, cols], in_=acc[:])
+
+        y_minus = sb.tile([P, S], F32, name="y_minus")
+        x_minus = sb.tile([P, S], F32, name="x_minus")
+        dy = sb.tile([P, S], F32, name="dy")
+        gy = sb.tile([P, S], F32, name="gy")
+        gy2 = sb.tile([P, S], F32, name="gy2")
+        ly_gy = sb.tile([P, S], F32, name="ly_gy")
+        nc.vector.tensor_copy(out=y_minus[:], in_=y[:].indirect(ym_t[:]))
+        nc.vector.tensor_tensor(out=dy[:], in0=y[:].indirect(yp_t[:]), in1=y_minus[:], op=ALU.subtract)
+        nc.vector.tensor_tensor(out=gy[:], in0=dy[:], in1=h[:], op=ALU.mult)
+        nc.vector.tensor_copy(out=x_minus[:], in_=y[:].indirect(xm_t[:]))
+        nc.scalar.activation(out=gy2[:], in_=gy[:], func=ACT.Square)
+        nc.scalar.activation(out=ly_gy[:], in_=gy[:], func=ACT.Copy, scale=ly_t[:])
+
+        def halves(name):
+            return [sb.tile([P, HALF], F32, name="%s%d" % (name, c)) for c in range(2)]
+
+        dx, gx, gx2, lit, ss, inv, up, diffuse, up2, res = (
+            halves(n) for n in ("dx", "gx", "gx2", "lit", "ss", "inv", "up", "diffuse", "up2", "res")
+        )
+        cs = [slice(c * HALF, (c + 1) * HALF) for c in range(2)]
+        for c in range(2):
+            nc.vector.tensor_tensor(
+                out=dx[c][:],
+                in0=y[:].indirect(xp_t[:, c * HALF // 16 : (c + 1) * HALF // 16]),
+                in1=x_minus[:, cs[c]],
+                op=ALU.subtract,
+            )
+        for c in range(2):
+            nc.vector.tensor_tensor(out=gx[c][:], in0=dx[c][:], in1=h[:, cs[c]], op=ALU.mult)
+            nc.scalar.activation(out=gx2[c][:], in_=gx[c][:], func=ACT.Square)
+        for c in range(2):
+            nc.vector.scalar_tensor_tensor(
+                out=lit[c][:], in0=gx[c][:], scalar=lx_t[:], in1=ly_gy[:, cs[c]], op0=ALU.mult, op1=ALU.add
+            )
+            nc.vector.scalar_tensor_tensor(
+                out=ss[c][:], in0=gx2[c][:], scalar=0.1, in1=gy2[:, cs[c]], op0=ALU.add, op1=ALU.add
+            )
+            nc.scalar.activation(out=inv[c][:], in_=ss[c][:], func=ACT.Abs_reciprocal_sqrt)
+        for c in range(2):
+            nc.vector.scalar_tensor_tensor(
+                out=up[c][:], in0=gy[:, cs[c]], scalar=0.0, in1=inv[c][:], op0=ALU.max, op1=ALU.mult
+            )
+            nc.scalar.activation(out=up2[c][:], in_=up[c][:], func=ACT.Square, scale=math.sqrt(0.3))
+            nc.vector.scalar_tensor_tensor(
+                out=diffuse[c][:], in0=lit[c][:], scalar=0.0, in1=inv[c][:], op0=ALU.max, op1=ALU.mult
+            )
+        for c in range(2):
+            nc.vector.tensor_tensor(out=res[c][:], in0=diffuse[c][:], in1=up2[c][:], op=ALU.add)
+            nc.sync.dma_start(out=out[:, cs[c]], in_=res[c][:])

@@ -47,13 +47,13 @@ def tile_picked_ysdfnr_shade_p_kernel(
         nc.vector.memset(zero_view[:, : T // 8], 0)
         nc.gpsimd.memset(zero_view[:, T // 8 :], 0)
         nc.sync.dma_start(out=offs_t[:], in_=offs)
-        nc.scalar.dma_start(out=w_raw[:], in_=w1.rearrange("(p j) m -> p j m", j=PACK))
-        nc.scalar.dma_start(out=words[:], in_=x_words[0].rearrange("p n t -> p (n t)").bitcast(I32))
+        nc.sync.dma_start(out=w_raw[:], in_=w1.rearrange("(p j) m -> p j m", j=PACK))
         for q in range(4):
             nc.sync.dma_start(
                 out=scales[32 * q : 32 * q + 4, :].bitcast(I32),
                 in_=x_scales[0, 4 * q : 4 * q + 4, :].bitcast(I32),
             )
+        nc.sync.dma_start(out=words[:], in_=x_words[0].rearrange("p n t -> p (n t)").bitcast(I32))
         nc.sync.dma_start(out=ym_t[:], in_=ym)
         nc.sync.dma_start(out=yp_t[:], in_=yp)
         nc.sync.dma_start(out=xm_t[:], in_=xm)
@@ -86,17 +86,23 @@ def tile_picked_ysdfnr_shade_p_kernel(
             nc.vector.tensor_copy(
                 out=g_words[:], in_=words[:].bitcast(U32).indirect(offs_t[:, c * HALF // 16 : (c + 1) * HALF // 16])
             )
-            acc = ps.tile([P, HALF], F32, name="acc%d" % c)
-            nc.tensor.matmul_mx(
-                out=acc[:],
-                lhsT=w_codes[:].bitcast(FP8X4),
-                lhsT_scale=w_scales[:],
-                rhs=g_words[:].bitcast(FP8X4),
-                rhs_scale=g_scales[:, cols],
-                start=True,
-                stop=True,
-            )
-            nc.scalar.copy(out=y[:, cols], in_=acc[:])
+            pieces = [(0, HALF)] if c == 0 else [(0, HALF // 2), (HALF // 2, HALF)]
+            for lo, hi in pieces:
+                acc = ps.tile([P, hi - lo], F32, name="acc%d_%d" % (c, lo))
+                ycols = slice(c * HALF + lo, c * HALF + hi)
+                nc.tensor.matmul_mx(
+                    out=acc[:],
+                    lhsT=w_codes[:].bitcast(FP8X4),
+                    lhsT_scale=w_scales[:],
+                    rhs=g_words[:, lo:hi].bitcast(FP8X4),
+                    rhs_scale=g_scales[:, ycols],
+                    start=True,
+                    stop=True,
+                )
+                if lo == 0:
+                    nc.scalar.copy(out=y[:, ycols], in_=acc[:])
+                else:
+                    nc.vector.tensor_copy(out=y[:, ycols], in_=acc[:])
 
         y_minus = sb.tile([P, S], F32, name="y_minus")
         x_minus = sb.tile([P, S], F32, name="x_minus")

@@ -1,4 +1,3 @@
-import math
 from contextlib import ExitStack
 
 import concourse.mybir as mybir
@@ -16,7 +15,13 @@ ACT = mybir.ActivationFunctionType
 P = 128
 K, T, S, N = 512, 2048, 512, 128
 PACK = 4
+PER_COLUMN = 16
+QUADRANT = 32
+ROWS = 4
 HALF = S // 2
+QUARTER = S // 4
+UNDER_ROOT = 0.1
+FROM_ABOVE = 0.3
 FLOPS = 2 * K * S * N
 
 
@@ -29,11 +34,14 @@ def tile_picked_ysdfnr_shade_p_kernel(
         sb = ctx.enter_context(tc.tile_pool(name="sb", bufs=1))
         ps = ctx.enter_context(tc.psum_pool(name="ps", bufs=1))
 
-        offs_t = lists.tile([P, S // 16], U16, name="offs_t")
-        ym_t = lists.tile([P, S // 16], U16, name="ym_t")
-        yp_t = lists.tile([P, S // 16], U16, name="yp_t")
-        xm_t = lists.tile([P, S // 16], U16, name="xm_t")
-        xp_t = lists.tile([P, S // 16], U16, name="xp_t")
+        offs_t = lists.tile([P, S // PER_COLUMN], U16, name="offs_t")
+        ym_t = lists.tile([P, S // PER_COLUMN], U16, name="ym_t")
+        yp_t = lists.tile([P, S // PER_COLUMN], U16, name="yp_t")
+        xm_t = lists.tile([P, S // PER_COLUMN], U16, name="xm_t")
+        xp_t = lists.tile([P, S // PER_COLUMN], U16, name="xp_t")
+
+        def entries(list_tile, c):
+            return list_tile[:, c * HALF // PER_COLUMN : (c + 1) * HALF // PER_COLUMN]
 
         scales = sb.tile([P, T], U8, name="scales", align_bytes=64)
         words = sb.tile([P, T], I32, name="words", align_bytes=64)
@@ -43,15 +51,16 @@ def tile_picked_ysdfnr_shade_p_kernel(
         ly_t = sb.tile([P, 1], F32, name="ly_t")
         y = sb.tile([P, 2 * S], F32, name="y")
 
-        zero_view = scales[:].bitcast(I32)
-        nc.vector.memset(zero_view[:, : T // 8], 0)
-        nc.gpsimd.memset(zero_view[:, T // 8 :], 0)
+        scale_words = scales[:].bitcast(I32)
+        nc.vector.memset(scale_words[:, : T // 8], 0)
+        nc.gpsimd.memset(scale_words[:, T // 8 :], 0)
+
         nc.sync.dma_start(out=offs_t[:], in_=offs)
         nc.sync.dma_start(out=w_raw[:], in_=w1.rearrange("(p j) m -> p j m", j=PACK))
-        for q in range(4):
+        for q in range(P // QUADRANT):
             nc.sync.dma_start(
-                out=scales[32 * q : 32 * q + 4, :].bitcast(I32),
-                in_=x_scales[0, 4 * q : 4 * q + 4, :].bitcast(I32),
+                out=scales[QUADRANT * q : QUADRANT * q + ROWS, :].bitcast(I32),
+                in_=x_scales[0, ROWS * q : ROWS * (q + 1), :].bitcast(I32),
             )
         nc.sync.dma_start(out=words[:], in_=x_words[0].rearrange("p n t -> p (n t)").bitcast(I32))
         nc.sync.dma_start(out=ym_t[:], in_=ym)
@@ -64,15 +73,15 @@ def tile_picked_ysdfnr_shade_p_kernel(
         nc.vector.memset(y[:, S:], 0.0)
 
         one = sb.tile([P, 1], F32, name="one")
-        warm = sb.tile([P, 1], F32, name="warm")
+        root_above = sb.tile([P, 1], F32, name="root_above")
         nc.vector.memset(one[:], 1.0)
-        nc.scalar.activation(out=warm[:], in_=one[:], func=ACT.Abs_reciprocal_sqrt)
+        nc.scalar.activation(out=root_above[:], in_=one[:], func=ACT.Abs_reciprocal_sqrt, scale=1.0 / FROM_ABOVE)
 
         w_bf = sb.tile([P, N, PACK], BF16, name="w_bf", align_bytes=64)
         nc.scalar.copy(out=w_bf[:], in_=w_raw[:].rearrange("p j m -> p m j"))
 
-        g_scales = sb.tile([P, S], U8, name="g_scales", align_bytes=64)
-        nc.vector.tensor_copy(out=g_scales[:], in_=scales[:].indirect(offs_t[:]))
+        picked_scales = sb.tile([P, S], U8, name="picked_scales", align_bytes=64)
+        nc.vector.tensor_copy(out=picked_scales[:], in_=scales[:].indirect(offs_t[:]))
 
         w_codes = sb.tile([P, N], U32, name="w_codes", align_bytes=64)
         w_scales = sb.tile([P, N], U8, name="w_scales", align_bytes=64)
@@ -80,29 +89,25 @@ def tile_picked_ysdfnr_shade_p_kernel(
             out=w_codes[:].bitcast(FP8X4), scales=w_scales[:], in_=w_bf[:].rearrange("p m j -> p (m j)")
         )
 
-        for c in range(2):
-            cols = slice(c * HALF, (c + 1) * HALF)
-            g_words = sb.tile([P, HALF], U32, name="g_words%d" % c, align_bytes=64)
-            nc.vector.tensor_copy(
-                out=g_words[:], in_=words[:].bitcast(U32).indirect(offs_t[:, c * HALF // 16 : (c + 1) * HALF // 16])
-            )
-            pieces = [(0, HALF)] if c == 0 else [(0, HALF // 2), (HALF // 2, HALF)]
-            for lo, hi in pieces:
+        for c, spans in enumerate(([(0, HALF)], [(0, QUARTER), (QUARTER, HALF)])):
+            picked_words = sb.tile([P, HALF], U32, name="picked_words%d" % c, align_bytes=64)
+            nc.vector.tensor_copy(out=picked_words[:], in_=words[:].bitcast(U32).indirect(entries(offs_t, c)))
+            for lo, hi in spans:
                 acc = ps.tile([P, hi - lo], F32, name="acc%d_%d" % (c, lo))
-                ycols = slice(c * HALF + lo, c * HALF + hi)
+                y_cols = slice(c * HALF + lo, c * HALF + hi)
                 nc.tensor.matmul_mx(
                     out=acc[:],
                     lhsT=w_codes[:].bitcast(FP8X4),
                     lhsT_scale=w_scales[:],
-                    rhs=g_words[:, lo:hi].bitcast(FP8X4),
-                    rhs_scale=g_scales[:, ycols],
+                    rhs=picked_words[:, lo:hi].bitcast(FP8X4),
+                    rhs_scale=picked_scales[:, y_cols],
                     start=True,
                     stop=True,
                 )
                 if lo == 0:
-                    nc.scalar.copy(out=y[:, ycols], in_=acc[:])
+                    nc.scalar.copy(out=y[:, y_cols], in_=acc[:])
                 else:
-                    nc.vector.tensor_copy(out=y[:, ycols], in_=acc[:])
+                    nc.vector.tensor_copy(out=y[:, y_cols], in_=acc[:])
 
         y_minus = sb.tile([P, S], F32, name="y_minus")
         x_minus = sb.tile([P, S], F32, name="x_minus")
@@ -115,41 +120,61 @@ def tile_picked_ysdfnr_shade_p_kernel(
         nc.vector.tensor_tensor(out=gy[:], in0=dy[:], in1=h[:], op=ALU.mult)
         nc.vector.tensor_copy(out=x_minus[:], in_=y[:].indirect(xm_t[:]))
         nc.scalar.activation(out=gy2[:], in_=gy[:], func=ACT.Square)
-        nc.scalar.activation(out=ly_gy[:], in_=gy[:], func=ACT.Copy, scale=ly_t[:])
+        nc.scalar.activation(out=ly_gy[:, :HALF], in_=gy[:, :HALF], func=ACT.Copy, scale=ly_t[:])
+
+        def piece(name, width, tag=None):
+            return sb.tile([P, width], F32, name=name, tag=tag or name)
 
         def halves(name):
-            return [sb.tile([P, HALF], F32, name="%s%d" % (name, c)) for c in range(2)]
+            return [piece("%s%d" % (name, c), HALF) for c in range(2)]
 
-        dx, gx, gx2, lit, ss, inv, up, diffuse, up2, res = (
-            halves(n) for n in ("dx", "gx", "gx2", "lit", "ss", "inv", "up", "diffuse", "up2", "res")
-        )
-        cs = [slice(c * HALF, (c + 1) * HALF) for c in range(2)]
+        def quarters(name):
+            return [piece("%s%d" % (name, q), QUARTER) for q in range(4)]
+
+        def quarter_of(half_tiles, q):
+            return half_tiles[q // 2][:, (q % 2) * QUARTER : (q % 2 + 1) * QUARTER]
+
+        dx, gx, inv, up, up2, res = (halves(n) for n in ("dx", "gx", "inv", "up", "up2", "res"))
+        gx2, sum2 = quarters("gx2_"), quarters("sum2_")
+        half_cols = [slice(c * HALF, (c + 1) * HALF) for c in range(2)]
+        quarter_cols = [slice(q * QUARTER, (q + 1) * QUARTER) for q in range(4)]
         for c in range(2):
             nc.vector.tensor_tensor(
-                out=dx[c][:],
-                in0=y[:].indirect(xp_t[:, c * HALF // 16 : (c + 1) * HALF // 16]),
-                in1=x_minus[:, cs[c]],
-                op=ALU.subtract,
+                out=dx[c][:], in0=y[:].indirect(entries(xp_t, c)), in1=x_minus[:, half_cols[c]], op=ALU.subtract
             )
-        for c in range(2):
-            nc.vector.tensor_tensor(out=gx[c][:], in0=dx[c][:], in1=h[:, cs[c]], op=ALU.mult)
-            nc.scalar.activation(out=gx2[c][:], in_=gx[c][:], func=ACT.Square)
+
+        for q in range(4):
+            nc.vector.tensor_tensor(
+                out=quarter_of(gx, q), in0=quarter_of(dx, q), in1=h[:, quarter_cols[q]], op=ALU.mult
+            )
+            nc.scalar.activation(out=gx2[q][:], in_=quarter_of(gx, q), func=ACT.Square)
+
+        def lit_half(c, tag):
+            lit_c = piece("lit%d" % c, HALF, tag)
+            nc.vector.scalar_tensor_tensor(
+                out=lit_c[:], in0=gx[c][:], scalar=lx_t[:], in1=ly_gy[:, half_cols[c]], op0=ALU.mult, op1=ALU.add
+            )
+            return lit_c
+
+        lit_first = lit_half(0, None)
+        nc.scalar.activation(out=ly_gy[:, HALF:], in_=gy[:, HALF:], func=ACT.Copy, scale=ly_t[:])
+        for q in range(4):
+            nc.vector.scalar_tensor_tensor(
+                out=sum2[q][:], in0=gx2[q][:], scalar=UNDER_ROOT, in1=gy2[:, quarter_cols[q]], op0=ALU.add, op1=ALU.add
+            )
+            nc.scalar.activation(out=quarter_of(inv, q), in_=sum2[q][:], func=ACT.Abs_reciprocal_sqrt)
+        lit = [lit_first, lit_half(1, "gx2_2")]
+
         for c in range(2):
             nc.vector.scalar_tensor_tensor(
-                out=lit[c][:], in0=gx[c][:], scalar=lx_t[:], in1=ly_gy[:, cs[c]], op0=ALU.mult, op1=ALU.add
+                out=up[c][:], in0=gy[:, half_cols[c]], scalar=0.0, in1=inv[c][:], op0=ALU.max, op1=ALU.mult
             )
-            nc.vector.scalar_tensor_tensor(
-                out=ss[c][:], in0=gx2[c][:], scalar=0.1, in1=gy2[:, cs[c]], op0=ALU.add, op1=ALU.add
-            )
-            nc.scalar.activation(out=inv[c][:], in_=ss[c][:], func=ACT.Abs_reciprocal_sqrt)
+            nc.scalar.activation(out=up2[c][:], in_=up[c][:], func=ACT.Square, scale=root_above[:])
+        diffuse = [piece("diffuse0", HALF, "sum2_3"), piece("diffuse1", HALF)]
         for c in range(2):
-            nc.vector.scalar_tensor_tensor(
-                out=up[c][:], in0=gy[:, cs[c]], scalar=0.0, in1=inv[c][:], op0=ALU.max, op1=ALU.mult
-            )
-            nc.scalar.activation(out=up2[c][:], in_=up[c][:], func=ACT.Square, scale=math.sqrt(0.3))
             nc.vector.scalar_tensor_tensor(
                 out=diffuse[c][:], in0=lit[c][:], scalar=0.0, in1=inv[c][:], op0=ALU.max, op1=ALU.mult
             )
         for c in range(2):
             nc.vector.tensor_tensor(out=res[c][:], in0=diffuse[c][:], in1=up2[c][:], op=ALU.add)
-            nc.sync.dma_start(out=out[:, cs[c]], in_=res[c][:])
+            nc.sync.dma_start(out=out[:, half_cols[c]], in_=res[c][:])

from contextlib import ExitStack

import concourse.mybir as mybir

F32 = mybir.dt.float32
BF16 = mybir.dt.bfloat16
I32 = mybir.dt.int32
U32 = mybir.dt.uint32
U16 = mybir.dt.uint16
U8 = mybir.dt.uint8
FP8X4 = mybir.dt.float8_e4m3fn_x4
ALU = mybir.AluOpType
ACT = mybir.ActivationFunctionType

P = 128
K, T, S, N = 512, 2048, 512, 128
PACK = 4
PER_COLUMN = 16
QUADRANT = 32
ROWS = 4
HALF = S // 2
QUARTER = S // 4
UNDER_ROOT = 0.1
FROM_ABOVE = 0.3
FLOPS = 2 * K * S * N


def tile_picked_ysdfnr_shade_p_kernel(
    tc, x_words, x_scales, w1, half, lx, ly, offs, xp, xm, yp, ym, out
):
    nc = tc.nc
    with ExitStack() as ctx:
        lists = ctx.enter_context(tc.tile_pool(name="lists", bufs=1))
        sb = ctx.enter_context(tc.tile_pool(name="sb", bufs=1))
        ps = ctx.enter_context(tc.psum_pool(name="ps", bufs=1))

        offs_t = lists.tile([P, S // PER_COLUMN], U16, name="offs_t")
        ym_t = lists.tile([P, S // PER_COLUMN], U16, name="ym_t")
        yp_t = lists.tile([P, S // PER_COLUMN], U16, name="yp_t")
        xm_t = lists.tile([P, S // PER_COLUMN], U16, name="xm_t")
        xp_t = lists.tile([P, S // PER_COLUMN], U16, name="xp_t")

        def entries(list_tile, c):
            return list_tile[:, c * HALF // PER_COLUMN : (c + 1) * HALF // PER_COLUMN]

        scales = sb.tile([P, T], U8, name="scales", align_bytes=64)
        words = sb.tile([P, T], I32, name="words", align_bytes=64)
        w_raw = sb.tile([P, PACK, N], F32, name="w_raw")
        h = sb.tile([P, S], F32, name="h")
        lx_t = sb.tile([P, 1], F32, name="lx_t")
        ly_t = sb.tile([P, 1], F32, name="ly_t")
        y = sb.tile([P, 2 * S], F32, name="y")

        scale_words = scales[:].bitcast(I32)
        nc.vector.memset(scale_words[:, : T // 8], 0)
        nc.gpsimd.memset(scale_words[:, T // 8 :], 0)

        nc.sync.dma_start(out=offs_t[:], in_=offs)
        nc.sync.dma_start(out=w_raw[:], in_=w1.rearrange("(p j) m -> p j m", j=PACK))
        for q in range(P // QUADRANT):
            nc.sync.dma_start(
                out=scales[QUADRANT * q : QUADRANT * q + ROWS, :].bitcast(I32),
                in_=x_scales[0, ROWS * q : ROWS * (q + 1), :].bitcast(I32),
            )
        nc.sync.dma_start(out=words[:], in_=x_words[0].rearrange("p n t -> p (n t)").bitcast(I32))
        nc.sync.dma_start(out=ym_t[:], in_=ym)
        nc.sync.dma_start(out=yp_t[:], in_=yp)
        nc.sync.dma_start(out=xm_t[:], in_=xm)
        nc.sync.dma_start(out=h[:], in_=half)
        nc.sync.dma_start(out=ly_t[:], in_=ly)
        nc.sync.dma_start(out=xp_t[:], in_=xp)
        nc.sync.dma_start(out=lx_t[:], in_=lx)
        nc.vector.memset(y[:, S:], 0.0)

        one = sb.tile([P, 1], F32, name="one")
        root_above = sb.tile([P, 1], F32, name="root_above")
        nc.vector.memset(one[:], 1.0)
        nc.scalar.activation(out=root_above[:], in_=one[:], func=ACT.Abs_reciprocal_sqrt, scale=1.0 / FROM_ABOVE)

        w_bf = sb.tile([P, N, PACK], BF16, name="w_bf", align_bytes=64)
        nc.scalar.copy(out=w_bf[:], in_=w_raw[:].rearrange("p j m -> p m j"))

        picked_scales = sb.tile([P, S], U8, name="picked_scales", align_bytes=64)
        nc.vector.tensor_copy(out=picked_scales[:], in_=scales[:].indirect(offs_t[:]))

        w_codes = sb.tile([P, N], U32, name="w_codes", align_bytes=64)
        w_scales = sb.tile([P, N], U8, name="w_scales", align_bytes=64)
        nc.vector.quantize_mx(
            out=w_codes[:].bitcast(FP8X4), scales=w_scales[:], in_=w_bf[:].rearrange("p m j -> p (m j)")
        )

        for c, spans in enumerate(([(0, HALF)], [(0, QUARTER), (QUARTER, HALF)])):
            picked_words = sb.tile([P, HALF], U32, name="picked_words%d" % c, align_bytes=64)
            nc.vector.tensor_copy(out=picked_words[:], in_=words[:].bitcast(U32).indirect(entries(offs_t, c)))
            for lo, hi in spans:
                acc = ps.tile([P, hi - lo], F32, name="acc%d_%d" % (c, lo))
                y_cols = slice(c * HALF + lo, c * HALF + hi)
                nc.tensor.matmul_mx(
                    out=acc[:],
                    lhsT=w_codes[:].bitcast(FP8X4),
                    lhsT_scale=w_scales[:],
                    rhs=picked_words[:, lo:hi].bitcast(FP8X4),
                    rhs_scale=picked_scales[:, y_cols],
                    start=True,
                    stop=True,
                )
                if lo == 0:
                    nc.scalar.copy(out=y[:, y_cols], in_=acc[:])
                else:
                    nc.vector.tensor_copy(out=y[:, y_cols], in_=acc[:])

        y_minus = sb.tile([P, S], F32, name="y_minus")
        x_minus = sb.tile([P, S], F32, name="x_minus")
        dy = sb.tile([P, S], F32, name="dy")
        gy = sb.tile([P, S], F32, name="gy")
        gy2 = sb.tile([P, S], F32, name="gy2")
        ly_gy = sb.tile([P, S], F32, name="ly_gy")
        nc.vector.tensor_copy(out=y_minus[:], in_=y[:].indirect(ym_t[:]))
        nc.vector.tensor_tensor(out=dy[:], in0=y[:].indirect(yp_t[:]), in1=y_minus[:], op=ALU.subtract)
        nc.vector.tensor_tensor(out=gy[:], in0=dy[:], in1=h[:], op=ALU.mult)
        nc.vector.tensor_copy(out=x_minus[:], in_=y[:].indirect(xm_t[:]))
        nc.scalar.activation(out=gy2[:], in_=gy[:], func=ACT.Square)
        nc.scalar.activation(out=ly_gy[:, :HALF], in_=gy[:, :HALF], func=ACT.Copy, scale=ly_t[:])

        def piece(name, width, tag=None):
            return sb.tile([P, width], F32, name=name, tag=tag or name)

        def halves(name):
            return [piece("%s%d" % (name, c), HALF) for c in range(2)]

        def quarters(name):
            return [piece("%s%d" % (name, q), QUARTER) for q in range(4)]

        def quarter_of(half_tiles, q):
            return half_tiles[q // 2][:, (q % 2) * QUARTER : (q % 2 + 1) * QUARTER]

        dx, gx, inv, up, up2, res = (halves(n) for n in ("dx", "gx", "inv", "up", "up2", "res"))
        gx2, sum2 = quarters("gx2_"), quarters("sum2_")
        half_cols = [slice(c * HALF, (c + 1) * HALF) for c in range(2)]
        quarter_cols = [slice(q * QUARTER, (q + 1) * QUARTER) for q in range(4)]
        for c in range(2):
            nc.vector.tensor_tensor(
                out=dx[c][:], in0=y[:].indirect(entries(xp_t, c)), in1=x_minus[:, half_cols[c]], op=ALU.subtract
            )

        for q in range(4):
            nc.vector.tensor_tensor(
                out=quarter_of(gx, q), in0=quarter_of(dx, q), in1=h[:, quarter_cols[q]], op=ALU.mult
            )
            nc.scalar.activation(out=gx2[q][:], in_=quarter_of(gx, q), func=ACT.Square)

        def lit_half(c, tag):
            lit_c = piece("lit%d" % c, HALF, tag)
            nc.vector.scalar_tensor_tensor(
                out=lit_c[:], in0=gx[c][:], scalar=lx_t[:], in1=ly_gy[:, half_cols[c]], op0=ALU.mult, op1=ALU.add
            )
            return lit_c

        lit_first = lit_half(0, None)
        nc.scalar.activation(out=ly_gy[:, HALF:], in_=gy[:, HALF:], func=ACT.Copy, scale=ly_t[:])
        for q in range(4):
            nc.vector.scalar_tensor_tensor(
                out=sum2[q][:], in0=gx2[q][:], scalar=UNDER_ROOT, in1=gy2[:, quarter_cols[q]], op0=ALU.add, op1=ALU.add
            )
            nc.scalar.activation(out=quarter_of(inv, q), in_=sum2[q][:], func=ACT.Abs_reciprocal_sqrt)
        lit = [lit_first, lit_half(1, "gx2_2")]

        for c in range(2):
            nc.vector.scalar_tensor_tensor(
                out=up[c][:], in0=gy[:, half_cols[c]], scalar=0.0, in1=inv[c][:], op0=ALU.max, op1=ALU.mult
            )
            nc.scalar.activation(out=up2[c][:], in_=up[c][:], func=ACT.Square, scale=root_above[:])
        diffuse = [piece("diffuse0", HALF, "sum2_3"), piece("diffuse1", HALF)]
        for c in range(2):
            nc.vector.scalar_tensor_tensor(
                out=diffuse[c][:], in0=lit[c][:], scalar=0.0, in1=inv[c][:], op0=ALU.max, op1=ALU.mult
            )
        for c in range(2):
            nc.vector.tensor_tensor(out=res[c][:], in0=diffuse[c][:], in1=up2[c][:], op=ALU.add)
            nc.sync.dma_start(out=out[:, half_cols[c]], in_=res[c][:])
